import numpy as np
import ml_dtypes

BF16 = ml_dtypes.bfloat16


def bf(x):
    return np.asarray(x, np.float32).astype(BF16)


def f32(x):
    return np.asarray(x, np.float32)


def f64(x):
    return np.asarray(x).astype(np.float64)


def striped(idx):
    return np.tile(idx.reshape(-1, 16).T, (8, 1))


S, K, M, N, E, Q = 512, 128, 256, 256, 4, 64


def setup_inputs():
    return {"base": bf(np.random.standard_normal((M, S))), "x": bf(np.random.standard_normal((K, N))), "w": bf(np.random.standard_normal((E, K, M)) / np.sqrt(K)), "b": f32(0.5 * np.random.standard_normal((M, 1))), "offs": striped(np.random.permutation(S)[:N])}


def reference(base, x, w, b, offs):
    idx = offs[:16].T.reshape(-1)
    z = f64(base).copy()
    for e in range(E):
        z[:, idx[e * Q : (e + 1) * Q]] += f64(w)[e].T @ f64(x)[:, e * Q : (e + 1) * Q]
    return np.maximum(z + f64(b), 0.0)

@@ -1,0 +1,65 @@
+import concourse.mybir as mybir
+from concourse.masks import make_identity
+
+BF16, F32, U16 = mybir.dt.bfloat16, mybir.dt.float32, mybir.dt.uint16
+ADD, MAX = mybir.AluOpType.add, mybir.AluOpType.max
+RELU = mybir.ActivationFunctionType.Relu
+
+P = 128
+TOKENS = 512
+FEATURES = 256
+BLOCKS = FEATURES // P
+EXPERTS = 4
+PIECE = 64
+ENTRIES = EXPERTS * PIECE
+PIECE_COLS = PIECE // 16
+
+FLOPS = 2 * P * FEATURES * ENTRIES
+
+
+def tile_scatter_matmul_kernel(tc, base, x, w, b, offs, out):
+    nc = tc.nc
+    with (
+        tc.tile_pool(name="held", bufs=1) as held,
+        tc.psum_pool(name="windows", bufs=1) as windows,
+    ):
+        offsets = held.tile([P, ENTRIES // 16], U16, name="offsets")
+        nc.sync.dma_start(offsets[:], offs)
+        base_rows = []
+        for a in range(BLOCKS):
+            rows = held.tile([P, TOKENS], BF16, name="base_rows%d" % a)
+            nc.sync.dma_start(rows[:], base[a * P : (a + 1) * P, :])
+            base_rows.append(rows)
+        x_all = held.tile([P, ENTRIES], BF16, name="x_all")
+        nc.scalar.dma_start(x_all[:], x)
+        w_all = held.tile([P, EXPERTS, FEATURES], BF16, name="w_all")
+        nc.scalar.dma_start(w_all[:], w.rearrange("e k m -> k e m"))
+        bias = held.tile([P, BLOCKS], F32, name="bias")
+        with nc.allow_non_contiguous_dma(reason="one float32 bias value to a partition"):
+            nc.scalar.dma_start(bias[:], b.rearrange("(a p) o -> p (a o)", p=P))
+
+        ident = held.tile([P, P], BF16, name="ident")
+        make_identity(nc, ident[:])
+
+        window = []
+        for a in range(BLOCKS):
+            bank = windows.tile([P, TOKENS], F32, name="window%d" % a)
+            nc.tensor.matmul(bank[:], ident[:], base_rows[a][:], start=True, stop=False)
+            window.append(bank)
+
+        result = []
+        for a in range(BLOCKS):
+            for e in range(EXPERTS):
+                nc.tensor.matmul(
+                    window[a][:].indirect(offsets[:, e * PIECE_COLS : (e + 1) * PIECE_COLS]),
+                    w_all[:, e, a * P : (a + 1) * P],
+                    x_all[:, e * PIECE : (e + 1) * PIECE],
+                    start=False,
+                    stop=(e == EXPERTS - 1),
+                )
+            result.append(held.tile([P, TOKENS], F32, name="result%d" % a))
+
+        nc.vector.tensor_scalar(result[0][:], window[0][:], bias[:, 0:1], 0.0, ADD, MAX)
+        nc.sync.dma_start(out[0:P, :], result[0][:])
+        nc.scalar.activation(result[1][:], window[1][:], RELU, bias=bias[:, 1:2])
+        nc.scalar.dma_start(out[P : 2 * P, :], result[1][:])

@@ -23,23 +23,29 @@ def tile_scatter_matmul_kernel(tc, base, x, w, b, offs, out):
         tc.tile_pool(name="held", bufs=1) as held,
         tc.psum_pool(name="windows", bufs=1) as windows,
     ):
-        offsets = held.tile([P, ENTRIES // 16], U16, name="offsets")
-        nc.sync.dma_start(offsets[:], offs)
+        queues = (nc.sync, nc.scalar)
         base_rows = []
         for a in range(BLOCKS):
             rows = held.tile([P, TOKENS], BF16, name="base_rows%d" % a)
-            nc.sync.dma_start(rows[:], base[a * P : (a + 1) * P, :])
+            queues[a % 2].dma_start(rows[:], base[a * P : (a + 1) * P, :])
             base_rows.append(rows)
+        offsets = held.tile([P, ENTRIES // 16], U16, name="offsets")
+        nc.sync.dma_start(offsets[:], offs)
         x_all = held.tile([P, ENTRIES], BF16, name="x_all")
         nc.scalar.dma_start(x_all[:], x)
-        w_all = held.tile([P, EXPERTS, FEATURES], BF16, name="w_all")
-        nc.scalar.dma_start(w_all[:], w.rearrange("e k m -> k e m"))
-        bias = held.tile([P, BLOCKS], F32, name="bias")
-        with nc.allow_non_contiguous_dma(reason="one float32 bias value to a partition"):
-            nc.scalar.dma_start(bias[:], b.rearrange("(a p) o -> p (a o)", p=P))
+        w_expert = []
+        for e in range(EXPERTS):
+            weights = held.tile([P, FEATURES], BF16, name="w_expert%d" % e)
+            queues[e % 2].dma_start(weights[:], w[e])
+            w_expert.append(weights)
 
         ident = held.tile([P, P], BF16, name="ident")
         make_identity(nc, ident[:])
+        unused = held.tile([P, 1], F32, name="unused")
+        nc.scalar.activation(unused[:], ident[:, 0:1], RELU)
+        bias = held.tile([P, BLOCKS], F32, name="bias")
+        with nc.allow_non_contiguous_dma(reason="one float32 bias value to a partition"):
+            nc.gpsimd.dma_start(bias[:], b.rearrange("(a p) o -> p (a o)", p=P))
 
         window = []
         for a in range(BLOCKS):
@@ -47,18 +53,17 @@ def tile_scatter_matmul_kernel(tc, base, x, w, b, offs, out):
             nc.tensor.matmul(bank[:], ident[:], base_rows[a][:], start=True, stop=False)
             window.append(bank)
 
-        result = []
         for a in range(BLOCKS):
             for e in range(EXPERTS):
                 nc.tensor.matmul(
                     window[a][:].indirect(offsets[:, e * PIECE_COLS : (e + 1) * PIECE_COLS]),
-                    w_all[:, e, a * P : (a + 1) * P],
+                    w_expert[e][:, a * P : (a + 1) * P],
                     x_all[:, e * PIECE : (e + 1) * PIECE],
                     start=False,
                     stop=(e == EXPERTS - 1),
                 )
-            result.append(held.tile([P, TOKENS], F32, name="result%d" % a))
 
+        result = [held.tile([P, TOKENS], F32, name="result%d" % a) for a in range(BLOCKS)]
         nc.vector.tensor_scalar(result[0][:], window[0][:], bias[:, 0:1], 0.0, ADD, MAX)
         nc.sync.dma_start(out[0:P, :], result[0][:])
         nc.scalar.activation(result[1][:], window[1][:], RELU, bias=bias[:, 1:2])

@@ -14,6 +14,8 @@ PIECE = 64
 ENTRIES = EXPERTS * PIECE
 PIECE_COLS = PIECE // 16
 
+WARM_UPS = 4
+
 FLOPS = 2 * P * FEATURES * ENTRIES
 
 
@@ -23,29 +25,29 @@ def tile_scatter_matmul_kernel(tc, base, x, w, b, offs, out):
         tc.tile_pool(name="held", bufs=1) as held,
         tc.psum_pool(name="windows", bufs=1) as windows,
     ):
-        queues = (nc.sync, nc.scalar)
+        zeros = held.tile([P, TOKENS], BF16, name="zeros")
+        nc.vector.memset(zeros[:], 0.0)
+        unread = windows.tile([P, TOKENS], F32, name="unread")
+        for i in range(WARM_UPS):
+            nc.tensor.matmul(unread[:], zeros[:, 0:P], zeros[:], start=True, stop=True)
+
+        offsets = held.tile([P, ENTRIES // 16], U16, name="offsets")
+        nc.sync.dma_start(offsets[:], offs)
         base_rows = []
         for a in range(BLOCKS):
             rows = held.tile([P, TOKENS], BF16, name="base_rows%d" % a)
-            queues[a % 2].dma_start(rows[:], base[a * P : (a + 1) * P, :])
+            nc.sync.dma_start(rows[:], base[a * P : (a + 1) * P, :])
             base_rows.append(rows)
-        offsets = held.tile([P, ENTRIES // 16], U16, name="offsets")
-        nc.sync.dma_start(offsets[:], offs)
         x_all = held.tile([P, ENTRIES], BF16, name="x_all")
         nc.scalar.dma_start(x_all[:], x)
-        w_expert = []
-        for e in range(EXPERTS):
-            weights = held.tile([P, FEATURES], BF16, name="w_expert%d" % e)
-            queues[e % 2].dma_start(weights[:], w[e])
-            w_expert.append(weights)
+        w_all = held.tile([P, EXPERTS, FEATURES], BF16, name="w_all")
+        nc.scalar.dma_start(w_all[:], w.rearrange("e k m -> k e m"))
+        bias = held.tile([P, BLOCKS], F32, name="bias")
+        with nc.allow_non_contiguous_dma(reason="one float32 bias value to a partition"):
+            nc.scalar.dma_start(bias[:], b.rearrange("(a p) o -> p (a o)", p=P))
 
         ident = held.tile([P, P], BF16, name="ident")
         make_identity(nc, ident[:])
-        unused = held.tile([P, 1], F32, name="unused")
-        nc.scalar.activation(unused[:], ident[:, 0:1], RELU)
-        bias = held.tile([P, BLOCKS], F32, name="bias")
-        with nc.allow_non_contiguous_dma(reason="one float32 bias value to a partition"):
-            nc.gpsimd.dma_start(bias[:], b.rearrange("(a p) o -> p (a o)", p=P))
 
         window = []
         for a in range(BLOCKS):
@@ -53,17 +55,18 @@ def tile_scatter_matmul_kernel(tc, base, x, w, b, offs, out):
             nc.tensor.matmul(bank[:], ident[:], base_rows[a][:], start=True, stop=False)
             window.append(bank)
 
+        result = []
         for a in range(BLOCKS):
             for e in range(EXPERTS):
                 nc.tensor.matmul(
                     window[a][:].indirect(offsets[:, e * PIECE_COLS : (e + 1) * PIECE_COLS]),
-                    w_expert[e][:, a * P : (a + 1) * P],
+                    w_all[:, e, a * P : (a + 1) * P],
                     x_all[:, e * PIECE : (e + 1) * PIECE],
                     start=False,
                     stop=(e == EXPERTS - 1),
                 )
+            result.append(held.tile([P, TOKENS], F32, name="result%d" % a))
 
-        result = [held.tile([P, TOKENS], F32, name="result%d" % a) for a in range(BLOCKS)]
         nc.vector.tensor_scalar(result[0][:], window[0][:], bias[:, 0:1], 0.0, ADD, MAX)
         nc.sync.dma_start(out[0:P, :], result[0][:])
         nc.scalar.activation(result[1][:], window[1][:], RELU, bias=bias[:, 1:2])

@@ -14,8 +14,6 @@ PIECE = 64
 ENTRIES = EXPERTS * PIECE
 PIECE_COLS = PIECE // 16
 
-WARM_UPS = 4
-
 FLOPS = 2 * P * FEATURES * ENTRIES
 
 
@@ -25,29 +23,23 @@ def tile_scatter_matmul_kernel(tc, base, x, w, b, offs, out):
         tc.tile_pool(name="held", bufs=1) as held,
         tc.psum_pool(name="windows", bufs=1) as windows,
     ):
-        zeros = held.tile([P, TOKENS], BF16, name="zeros")
-        nc.vector.memset(zeros[:], 0.0)
-        unread = windows.tile([P, TOKENS], F32, name="unread")
-        for i in range(WARM_UPS):
-            nc.tensor.matmul(unread[:], zeros[:, 0:P], zeros[:], start=True, stop=True)
-
+        base_rows = [held.tile([P, TOKENS], BF16, name="base_rows%d" % a) for a in range(BLOCKS)]
+        nc.sync.dma_start(base_rows[0][:], base[0:P, :])
+        nc.scalar.dma_start(base_rows[1][:], base[P : 2 * P, :])
         offsets = held.tile([P, ENTRIES // 16], U16, name="offsets")
         nc.sync.dma_start(offsets[:], offs)
-        base_rows = []
-        for a in range(BLOCKS):
-            rows = held.tile([P, TOKENS], BF16, name="base_rows%d" % a)
-            nc.sync.dma_start(rows[:], base[a * P : (a + 1) * P, :])
-            base_rows.append(rows)
-        x_all = held.tile([P, ENTRIES], BF16, name="x_all")
-        nc.scalar.dma_start(x_all[:], x)
         w_all = held.tile([P, EXPERTS, FEATURES], BF16, name="w_all")
         nc.scalar.dma_start(w_all[:], w.rearrange("e k m -> k e m"))
+        x_all = held.tile([P, ENTRIES], BF16, name="x_all")
+        nc.sync.dma_start(x_all[:], x)
         bias = held.tile([P, BLOCKS], F32, name="bias")
         with nc.allow_non_contiguous_dma(reason="one float32 bias value to a partition"):
-            nc.scalar.dma_start(bias[:], b.rearrange("(a p) o -> p (a o)", p=P))
+            nc.sync.dma_start(bias[:], b.rearrange("(a p) o -> p (a o)", p=P))
 
         ident = held.tile([P, P], BF16, name="ident")
         make_identity(nc, ident[:])
+        unread_column = held.tile([P, 1], F32, name="unread_column")
+        nc.scalar.activation(unread_column[:], ident[:, 0:1], RELU)
 
         window = []
         for a in range(BLOCKS):
@@ -55,7 +47,6 @@ def tile_scatter_matmul_kernel(tc, base, x, w, b, offs, out):
             nc.tensor.matmul(bank[:], ident[:], base_rows[a][:], start=True, stop=False)
             window.append(bank)
 
-        result = []
         for a in range(BLOCKS):
             for e in range(EXPERTS):
                 nc.tensor.matmul(
@@ -65,8 +56,8 @@ def tile_scatter_matmul_kernel(tc, base, x, w, b, offs, out):
                     start=False,
                     stop=(e == EXPERTS - 1),
                 )
-            result.append(held.tile([P, TOKENS], F32, name="result%d" % a))
 
+        result = [held.tile([P, TOKENS], F32, name="result%d" % a) for a in range(BLOCKS)]
         nc.vector.tensor_scalar(result[0][:], window[0][:], bias[:, 0:1], 0.0, ADD, MAX)
         nc.sync.dma_start(out[0:P, :], result[0][:])
         nc.scalar.activation(result[1][:], window[1][:], RELU, bias=bias[:, 1:2])

@@ -14,6 +14,8 @@ PIECE = 64
 ENTRIES = EXPERTS * PIECE
 PIECE_COLS = PIECE // 16
 
+WARM_UPS = 2
+
 FLOPS = 2 * P * FEATURES * ENTRIES
 
 
@@ -35,6 +37,12 @@ def tile_scatter_matmul_kernel(tc, base, x, w, b, offs, out):
         bias = held.tile([P, BLOCKS], F32, name="bias")
         with nc.allow_non_contiguous_dma(reason="one float32 bias value to a partition"):
             nc.sync.dma_start(bias[:], b.rearrange("(a p) o -> p (a o)", p=P))
+
+        zeros = held.tile([P, TOKENS], BF16, name="zeros")
+        nc.vector.memset(zeros[:], 0.0)
+        unread_bank = windows.tile([P, TOKENS], F32, name="unread_bank")
+        for i in range(WARM_UPS):
+            nc.tensor.matmul(unread_bank[:], zeros[:, 0:P], zeros[:], start=True, stop=True)
 
         ident = held.tile([P, P], BF16, name="ident")
         make_identity(nc, ident[:])

@@ -66,7 +66,7 @@ def tile_scatter_matmul_kernel(tc, base, x, w, b, offs, out):
                 )
 
         result = [held.tile([P, TOKENS], F32, name="result%d" % a) for a in range(BLOCKS)]
-        nc.vector.tensor_scalar(result[0][:], window[0][:], bias[:, 0:1], 0.0, ADD, MAX)
-        nc.sync.dma_start(out[0:P, :], result[0][:])
-        nc.scalar.activation(result[1][:], window[1][:], RELU, bias=bias[:, 1:2])
-        nc.scalar.dma_start(out[P : 2 * P, :], result[1][:])
+        nc.scalar.activation(result[0][:], window[0][:], RELU, bias=bias[:, 0:1])
+        nc.scalar.dma_start(out[0:P, :], result[0][:])
+        nc.vector.tensor_scalar(result[1][:], window[1][:], bias[:, 1:2], 0.0, ADD, MAX)
+        nc.sync.dma_start(out[P : 2 * P, :], result[1][:])

@@ -30,13 +30,14 @@ def tile_scatter_matmul_kernel(tc, base, x, w, b, offs, out):
         nc.scalar.dma_start(base_rows[1][:], base[P : 2 * P, :])
         offsets = held.tile([P, ENTRIES // 16], U16, name="offsets")
         nc.sync.dma_start(offsets[:], offs)
-        w_all = held.tile([P, EXPERTS, FEATURES], BF16, name="w_all")
-        nc.scalar.dma_start(w_all[:], w.rearrange("e k m -> k e m"))
+        w_block = [held.tile([P, EXPERTS, P], BF16, name="w_block%d" % a) for a in range(BLOCKS)]
+        nc.scalar.dma_start(w_block[0][:], w[:, :, 0:P].rearrange("e k m -> k e m"))
         x_all = held.tile([P, ENTRIES], BF16, name="x_all")
         nc.sync.dma_start(x_all[:], x)
+        nc.sync.dma_start(w_block[1][:], w[:, :, P : 2 * P].rearrange("e k m -> k e m"))
         bias = held.tile([P, BLOCKS], F32, name="bias")
         with nc.allow_non_contiguous_dma(reason="one float32 bias value to a partition"):
-            nc.sync.dma_start(bias[:], b.rearrange("(a p) o -> p (a o)", p=P))
+            nc.scalar.dma_start(bias[:], b.rearrange("(a p) o -> p (a o)", p=P))
 
         zeros = held.tile([P, TOKENS], BF16, name="zeros")
         nc.vector.memset(zeros[:], 0.0)
@@ -59,7 +60,7 @@ def tile_scatter_matmul_kernel(tc, base, x, w, b, offs, out):
             for e in range(EXPERTS):
                 nc.tensor.matmul(
                     window[a][:].indirect(offsets[:, e * PIECE_COLS : (e + 1) * PIECE_COLS]),
-                    w_all[:, e, a * P : (a + 1) * P],
+                    w_block[a][:, e, :],
                     x_all[:, e * PIECE : (e + 1) * PIECE],
                     start=False,
                     stop=(e == EXPERTS - 1),

@@ -26,18 +26,18 @@ def tile_scatter_matmul_kernel(tc, base, x, w, b, offs, out):
         tc.psum_pool(name="windows", bufs=1) as windows,
     ):
         base_rows = [held.tile([P, TOKENS], BF16, name="base_rows%d" % a) for a in range(BLOCKS)]
-        nc.sync.dma_start(base_rows[0][:], base[0:P, :])
-        nc.scalar.dma_start(base_rows[1][:], base[P : 2 * P, :])
+        for a in range(BLOCKS):
+            nc.sync.dma_start(base_rows[a][:], base[a * P : (a + 1) * P, :])
         offsets = held.tile([P, ENTRIES // 16], U16, name="offsets")
         nc.sync.dma_start(offsets[:], offs)
-        w_block = [held.tile([P, EXPERTS, P], BF16, name="w_block%d" % a) for a in range(BLOCKS)]
-        nc.scalar.dma_start(w_block[0][:], w[:, :, 0:P].rearrange("e k m -> k e m"))
         x_all = held.tile([P, ENTRIES], BF16, name="x_all")
         nc.sync.dma_start(x_all[:], x)
-        nc.sync.dma_start(w_block[1][:], w[:, :, P : 2 * P].rearrange("e k m -> k e m"))
+        w_block = [held.tile([P, EXPERTS, P], BF16, name="w_block%d" % a) for a in range(BLOCKS)]
+        for a in range(BLOCKS):
+            nc.sync.dma_start(w_block[a][:], w[:, :, a * P : (a + 1) * P].rearrange("e k m -> k e m"))
         bias = held.tile([P, BLOCKS], F32, name="bias")
         with nc.allow_non_contiguous_dma(reason="one float32 bias value to a partition"):
-            nc.scalar.dma_start(bias[:], b.rearrange("(a p) o -> p (a o)", p=P))
+            nc.sync.dma_start(bias[:], b.rearrange("(a p) o -> p (a o)", p=P))
 
         zeros = held.tile([P, TOKENS], BF16, name="zeros")
         nc.vector.memset(zeros[:], 0.0)

@@ -14,7 +14,7 @@ PIECE = 64
 ENTRIES = EXPERTS * PIECE
 PIECE_COLS = PIECE // 16
 
-WARM_UPS = 2
+WARM_UPS = 8
 
 FLOPS = 2 * P * FEATURES * ENTRIES
 
@@ -39,11 +39,11 @@ def tile_scatter_matmul_kernel(tc, base, x, w, b, offs, out):
         with nc.allow_non_contiguous_dma(reason="one float32 bias value to a partition"):
             nc.sync.dma_start(bias[:], b.rearrange("(a p) o -> p (a o)", p=P))
 
-        zeros = held.tile([P, TOKENS], BF16, name="zeros")
-        nc.vector.memset(zeros[:], 0.0)
-        unread_bank = windows.tile([P, TOKENS], F32, name="unread_bank")
+        zeros = held.tile([P, P], BF16, name="zeros")
+        nc.gpsimd.memset(zeros[:], 0.0)
+        unread_bank = windows.tile([P, P], F32, name="unread_bank")
         for i in range(WARM_UPS):
-            nc.tensor.matmul(unread_bank[:], zeros[:, 0:P], zeros[:], start=True, stop=True)
+            nc.tensor.matmul(unread_bank[:], zeros[:], zeros[:], start=True, stop=True)
 
         ident = held.tile([P, P], BF16, name="ident")
         make_identity(nc, ident[:])

@@ -13,6 +13,7 @@ EXPERTS = 4
 PIECE = 64
 ENTRIES = EXPERTS * PIECE
 PIECE_COLS = PIECE // 16
+HALF = EXPERTS // 2
 
 WARM_UPS = 8
 
@@ -32,9 +33,9 @@ def tile_scatter_matmul_kernel(tc, base, x, w, b, offs, out):
         nc.sync.dma_start(offsets[:], offs)
         x_all = held.tile([P, ENTRIES], BF16, name="x_all")
         nc.sync.dma_start(x_all[:], x)
-        w_block = [held.tile([P, EXPERTS, P], BF16, name="w_block%d" % a) for a in range(BLOCKS)]
-        for a in range(BLOCKS):
-            nc.sync.dma_start(w_block[a][:], w[:, :, a * P : (a + 1) * P].rearrange("e k m -> k e m"))
+        w_half = [held.tile([P, HALF, FEATURES], BF16, name="w_half%d" % h) for h in range(2)]
+        for h in range(2):
+            nc.sync.dma_start(w_half[h][:], w[h * HALF : (h + 1) * HALF].rearrange("e k m -> k e m"))
         bias = held.tile([P, BLOCKS], F32, name="bias")
         with nc.allow_non_contiguous_dma(reason="one float32 bias value to a partition"):
             nc.sync.dma_start(bias[:], b.rearrange("(a p) o -> p (a o)", p=P))
@@ -60,7 +61,7 @@ def tile_scatter_matmul_kernel(tc, base, x, w, b, offs, out):
             for e in range(EXPERTS):
                 nc.tensor.matmul(
                     window[a][:].indirect(offsets[:, e * PIECE_COLS : (e + 1) * PIECE_COLS]),
-                    w_block[a][:, e, :],
+                    w_half[e // HALF][:, e % HALF, a * P : (a + 1) * P],
                     x_all[:, e * PIECE : (e + 1) * PIECE],
                     start=False,
                     stop=(e == EXPERTS - 1),

@@ -68,7 +68,9 @@ def tile_scatter_matmul_kernel(tc, base, x, w, b, offs, out):
                 )
 
         result = [held.tile([P, TOKENS], F32, name="result%d" % a) for a in range(BLOCKS)]
-        nc.scalar.activation(result[0][:], window[0][:], RELU, bias=bias[:, 0:1])
-        nc.scalar.dma_start(out[0:P, :], result[0][:])
+        halves = [slice(h * TOKENS // 2, (h + 1) * TOKENS // 2) for h in range(2)]
+        for half in halves:
+            nc.scalar.activation(result[0][:, half], window[0][:, half], RELU, bias=bias[:, 0:1])
+            nc.scalar.dma_start(out[0:P, half], result[0][:, half])
         nc.vector.tensor_scalar(result[1][:], window[1][:], bias[:, 1:2], 0.0, ADD, MAX)
         nc.sync.dma_start(out[P : 2 * P, :], result[1][:])

@@ -57,15 +57,18 @@ def tile_scatter_matmul_kernel(tc, base, x, w, b, offs, out):
             nc.tensor.matmul(bank[:], ident[:], base_rows[a][:], start=True, stop=False)
             window.append(bank)
 
-        for a in range(BLOCKS):
-            for e in range(EXPERTS):
-                nc.tensor.matmul(
-                    window[a][:].indirect(offsets[:, e * PIECE_COLS : (e + 1) * PIECE_COLS]),
-                    w_half[e // HALF][:, e % HALF, a * P : (a + 1) * P],
-                    x_all[:, e * PIECE : (e + 1) * PIECE],
-                    start=False,
-                    stop=(e == EXPERTS - 1),
-                )
+        run = [(0, e) for e in range(HALF)]
+        run += [(1, 0)]
+        run += [(0, e) for e in range(HALF, EXPERTS)]
+        run += [(1, e) for e in range(1, EXPERTS)]
+        for a, e in run:
+            nc.tensor.matmul(
+                window[a][:].indirect(offsets[:, e * PIECE_COLS : (e + 1) * PIECE_COLS]),
+                w_half[e // HALF][:, e % HALF, a * P : (a + 1) * P],
+                x_all[:, e * PIECE : (e + 1) * PIECE],
+                start=False,
+                stop=(e == EXPERTS - 1),
+            )
 
         result = [held.tile([P, TOKENS], F32, name="result%d" % a) for a in range(BLOCKS)]
         halves = [slice(h * TOKENS // 2, (h + 1) * TOKENS // 2) for h in range(2)]

import concourse.mybir as mybir
from concourse.masks import make_identity

BF16, F32, U16 = mybir.dt.bfloat16, mybir.dt.float32, mybir.dt.uint16
ADD, MAX = mybir.AluOpType.add, mybir.AluOpType.max
RELU = mybir.ActivationFunctionType.Relu

P = 128
TOKENS = 512
FEATURES = 256
BLOCKS = FEATURES // P
EXPERTS = 4
PIECE = 64
ENTRIES = EXPERTS * PIECE
PIECE_COLS = PIECE // 16
HALF = EXPERTS // 2

WARM_UPS = 8

FLOPS = 2 * P * FEATURES * ENTRIES


def tile_scatter_matmul_kernel(tc, base, x, w, b, offs, out):
    nc = tc.nc
    with (
        tc.tile_pool(name="held", bufs=1) as held,
        tc.psum_pool(name="windows", bufs=1) as windows,
    ):
        base_rows = [held.tile([P, TOKENS], BF16, name="base_rows%d" % a) for a in range(BLOCKS)]
        for a in range(BLOCKS):
            nc.sync.dma_start(base_rows[a][:], base[a * P : (a + 1) * P, :])
        offsets = held.tile([P, ENTRIES // 16], U16, name="offsets")
        nc.sync.dma_start(offsets[:], offs)
        x_all = held.tile([P, ENTRIES], BF16, name="x_all")
        nc.sync.dma_start(x_all[:], x)
        w_half = [held.tile([P, HALF, FEATURES], BF16, name="w_half%d" % h) for h in range(2)]
        for h in range(2):
            nc.sync.dma_start(w_half[h][:], w[h * HALF : (h + 1) * HALF].rearrange("e k m -> k e m"))
        bias = held.tile([P, BLOCKS], F32, name="bias")
        with nc.allow_non_contiguous_dma(reason="one float32 bias value to a partition"):
            nc.sync.dma_start(bias[:], b.rearrange("(a p) o -> p (a o)", p=P))

        zeros = held.tile([P, P], BF16, name="zeros")
        nc.gpsimd.memset(zeros[:], 0.0)
        unread_bank = windows.tile([P, P], F32, name="unread_bank")
        for i in range(WARM_UPS):
            nc.tensor.matmul(unread_bank[:], zeros[:], zeros[:], start=True, stop=True)

        ident = held.tile([P, P], BF16, name="ident")
        make_identity(nc, ident[:])
        unread_column = held.tile([P, 1], F32, name="unread_column")
        nc.scalar.activation(unread_column[:], ident[:, 0:1], RELU)

        window = []
        for a in range(BLOCKS):
            bank = windows.tile([P, TOKENS], F32, name="window%d" % a)
            nc.tensor.matmul(bank[:], ident[:], base_rows[a][:], start=True, stop=False)
            window.append(bank)

        run = [(0, e) for e in range(HALF)]
        run += [(1, 0)]
        run += [(0, e) for e in range(HALF, EXPERTS)]
        run += [(1, e) for e in range(1, EXPERTS)]
        for a, e in run:
            nc.tensor.matmul(
                window[a][:].indirect(offsets[:, e * PIECE_COLS : (e + 1) * PIECE_COLS]),
                w_half[e // HALF][:, e % HALF, a * P : (a + 1) * P],
                x_all[:, e * PIECE : (e + 1) * PIECE],
                start=False,
                stop=(e == EXPERTS - 1),
            )

        result = [held.tile([P, TOKENS], F32, name="result%d" % a) for a in range(BLOCKS)]
        halves = [slice(h * TOKENS // 2, (h + 1) * TOKENS // 2) for h in range(2)]
        for half in halves:
            nc.scalar.activation(result[0][:, half], window[0][:, half], RELU, bias=bias[:, 0:1])
            nc.scalar.dma_start(out[0:P, half], result[0][:, half])
        nc.vector.tensor_scalar(result[1][:], window[1][:], bias[:, 1:2], 0.0, ADD, MAX)
        nc.sync.dma_start(out[P : 2 * P, :], result[1][:])
